import numpy as np
import ml_dtypes


def mxq(x, axis, fmt="e4m3"):
    dtype, down = {"e4m3": (ml_dtypes.float8_e4m3fn, 7), "e5m2": (ml_dtypes.float8_e5m2, 14)}[fmt]
    v = np.moveaxis(np.asarray(x, np.float32).astype(ml_dtypes.bfloat16).astype(np.float64), axis, -1)
    blocks = v.reshape(v.shape[:-1] + (-1, 32))
    amax = np.abs(blocks).max(-1, keepdims=True)
    byte = np.maximum(np.where(amax > 0, np.frexp(amax)[1] - 1 + 127, 0) - down, 1)
    scale = np.exp2(byte - 127.0)
    codes = (blocks / scale).astype(np.float32).astype(dtype).astype(np.float64)
    return np.moveaxis((codes * scale).reshape(v.shape), -1, axis)


WIDE = False


def mx_kscale(k):
    if not WIDE:
        return np.ones(k)
    levels = np.array([10, -10, 5, -5, 0])
    if k % 512:
        return np.exp2(np.random.permutation(np.resize(levels, k // 32))).repeat(32)
    a = np.empty((k // 512, 16))
    for p in range(k // 512):
        a[p, :8] = np.random.permutation(np.resize(levels, 8))
        for g in range(8):
            far = levels[np.abs(levels - a[p, g]) >= 10]
            a[p, g + 8] = far[np.random.randint(len(far))]
    return np.exp2(a.ravel()).repeat(32)


def f64(x):
    return np.asarray(x).astype(np.float64)


def striped(idx):
    return np.tile(np.asarray(idx).reshape(-1, 16).T, (8, 1)).astype(np.uint16)


def unstriped(offs):
    return offs[:16].T.reshape(-1).astype(np.int64)


E2M1 = np.array([0.0, 0.5, 1.0, 1.5, 2.0, 3.0, 4.0, 6.0, -0.0, -0.5, -1.0, -1.5, -2.0, -3.0, -4.0, -6.0])


def pack_weight(w, fmt):
    k, n = w.shape
    w = f64(np.asarray(w, np.float32).astype(ml_dtypes.bfloat16)).reshape(k // 32, 32, n)
    amax = np.abs(w).max(1)
    if fmt == "e4m3":
        byte = np.frexp(amax)[1] - 1 + 127 - 7
    else:
        mant, ex = np.frexp(amax / 6.0)
        byte = np.where(mant > 0.5, ex, ex - 1) + 127
    byte = np.clip(np.where(amax > 0, byte, 1), 1, 254)
    scaled = (w * np.exp2(127.0 - byte)[:, None, :]).reshape(k, n).astype(np.float32)
    by_word = np.ascontiguousarray(scaled.reshape(k // 512, 128, 4, n).transpose(0, 1, 3, 2))
    if fmt == "e4m3":
        words = by_word.astype(ml_dtypes.float8_e4m3fn).view(np.uint8)
    else:
        c = by_word.astype(ml_dtypes.float4_e2m1fn).view(np.uint8) & 0xF
        words = (c[..., 0::2] | (c[..., 1::2] << 4)).reshape(k // 512, 128, 2 * n)
    return np.ascontiguousarray(words), np.ascontiguousarray(byte.astype(np.uint8).reshape(k // 512, 16, n))


def unpack_weight(words, scales, fmt):
    g, _, n = scales.shape
    words = np.ascontiguousarray(words).reshape(g, 128, n, -1)
    if fmt == "e4m3":
        vals = words.view(ml_dtypes.float8_e4m3fn).astype(np.float64)
    else:
        nib = np.empty((g, 128, n, 4), np.uint8)
        nib[..., 0::2] = words & 0xF
        nib[..., 1::2] = words >> 4
        vals = E2M1[nib]
    vals = vals * np.repeat(np.exp2(scales.astype(np.float64) - 127.0), 8, axis=1)[..., None]
    return vals.transpose(0, 1, 3, 2).reshape(g * 512, n)


def bf(x):
    return np.asarray(x, np.float32).astype(ml_dtypes.bfloat16)


def planes(Y):
    r, m = Y.shape
    b = f64(bf(Y)).reshape(r // 32, 32, m)
    amax = np.abs(b).max(1)
    byte = np.clip(np.where(amax > 0, np.frexp(amax)[1] - 1 + 127 - 7, 1), 1, 254)
    codes = (b * np.exp2(127.0 - byte)[:, None, :]).reshape(r, m).astype(np.float32).astype(ml_dtypes.float8_e4m3fn).view(np.uint8)
    words = codes.reshape(r // 512, 128, 4, m).transpose(0, 1, 3, 2)
    return np.ascontiguousarray(words), np.ascontiguousarray(byte.astype(np.uint8).reshape(r // 512, 16, m))


D, E, T, I, Q = 512, 512, 1024, 256, 512


def setup_inputs():
    n = np.random.standard_normal
    idx = np.random.permutation(T)[:I]
    fd = mx_kscale(D)
    fq = mx_kscale(Q)
    keysp = pack_weight(n((D, T)) / fd[:, None], "e4m3")
    return {
        "query": (n((D, Q)) * 0.5 / np.sqrt(D) * fd[:, None]).astype(np.float32),
        "qs": (np.random.uniform(8.0, 32.0, (Q, 1)) * fq[:, None]).astype(np.float32),
        "grows": (n((Q, E)) / fq[:, None]).astype(np.float32),
        "vals": (n((E, T))).astype(np.float32),
        "keys_words": keysp[0],
        "keys_scales": keysp[1],
        "gain": (np.random.uniform(0.5, 2.0, (E, 1))).astype(np.float32),
        "sg": (np.random.uniform(0.5, 2.0, (1, I))).astype(np.float32),
        "old": (0.5 * n((E, I))).astype(np.float32),
        "offs": striped(idx),
    }


def reference(query, qs, grows, vals, keys_words, keys_scales, gain, sg, old, offs):
    idx = unstriped(offs)
    keysu = unpack_weight(keys_words, keys_scales, "e4m3")
    queryq = mxq(f64(query), 0, "e4m3")
    keysidxg = keysu[:, idx]
    a = queryq.T @ keysidxg
    p = np.exp(a - np.max(a, axis=1, keepdims=True))
    w = p * f64(qs) / np.sum(p, axis=1, keepdims=True)
    growsq = mxq(f64(grows), 0, "e4m3")
    wq = mxq(w, 0, "e4m3")
    c0 = growsq.T @ wq
    x1 = f64(vals)[:, idx] * f64(gain)
    vp = np.tanh(x1)
    dx1 = c0 * (1.0 - np.square(vp))
    y = dx1 * f64(sg) + f64(old)
    words, scales = planes(y)
    return y, words, scales

@@ -1,0 +1,215 @@
+from contextlib import ExitStack
+
+import concourse.mybir as mybir
+from concourse.masks import make_identity
+
+D, E, T, I, Q = 512, 512, 1024, 256, 512
+FLOPS = 2 * D * Q * I + 2 * Q * E * I
+
+F32 = mybir.dt.float32
+BF16 = mybir.dt.bfloat16
+I32 = mybir.dt.int32
+U32 = mybir.dt.uint32
+U16 = mybir.dt.uint16
+U8 = mybir.dt.uint8
+FP8X4 = mybir.dt.float8_e4m3fn_x4
+ALU = mybir.AluOpType
+ACT = mybir.ActivationFunctionType
+AX = mybir.AxisListType
+
+P = 128
+PACK = 4
+QUERY_SPLIT = 84
+GROWS_SPLIT = 24
+OUT_SPLIT = 42
+
+
+def deal(copy, dst, src, lo, hi):
+    copy(
+        out=dst[:].rearrange("p (r s j) -> p s r j", r=PACK, j=PACK)[:, lo:hi],
+        in_=src[:].rearrange("p j (s r) -> p s r j", r=PACK)[:, lo:hi],
+    )
+
+
+def tile_attend_bvtanh_d_pl_kernel(tc, query, qs, grows, vals, keys_words, keys_scales, gain, sg, old, offs, out_0, out_1, out_2):
+    nc = tc.nc
+    with ExitStack() as ctx:
+        sb = ctx.enter_context(tc.tile_pool(name="sb", bufs=1))
+        ps = ctx.enter_context(tc.psum_pool(name="ps", bufs=1))
+
+        k_bytes = sb.tile([P, T], U8, name="k_bytes", align_bytes=64)
+        nc.gpsimd.memset(k_bytes[:].bitcast(I32), 0)
+        offsets = sb.tile([P, I // 16], U16, name="offsets")
+        nc.sync.dma_start(offsets[:], offs)
+        for quad in range(4):
+            nc.scalar.dma_start(
+                out=k_bytes[32 * quad : 32 * quad + 4, :].bitcast(I32),
+                in_=keys_scales[0, 4 * quad : 4 * quad + 4, :].bitcast(I32),
+            )
+        q_raw = sb.tile([P, PACK, Q], F32, name="q_raw")
+        nc.sync.dma_start(out=q_raw[:], in_=query.rearrange("(p j) q -> p j q", j=PACK))
+        k_words = sb.tile([P, T], I32, name="k_words", align_bytes=64)
+        nc.sync.dma_start(out=k_words[:], in_=keys_words[0].rearrange("p n t -> p (n t)").bitcast(I32))
+
+        warm = sb.tile([P, 1], F32, name="warm")
+        warm2 = sb.tile([P, 1], F32, name="warm2")
+        nc.vector.memset(warm[:], 0.0)
+        nc.scalar.activation(out=warm2[:], in_=warm[:], func=ACT.Exp)
+
+        gain_sb = sb.tile([P, PACK], F32, name="gain_sb")
+        nc.gpsimd.dma_start(out=gain_sb[:], in_=gain.rearrange("(p t) o -> p (t o)", t=PACK))
+        qs_sb = sb.tile([P, PACK], F32, name="qs_sb")
+        nc.gpsimd.dma_start(out=qs_sb[:], in_=qs.rearrange("(p r) o -> p (r o)", r=PACK))
+        sg_cols = sb.tile([P, 2], F32, name="sg_cols")
+        nc.gpsimd.dma_start(out=sg_cols[:], in_=sg.rearrange("o (n m) -> n (o m)", m=2))
+
+        vals_planes = vals.rearrange("(p t) x -> t p x", t=PACK)
+        v_pool = [sb.tile([P, T], F32, name=f"v_pool{t}") for t in range(PACK)]
+        g_raw = sb.tile([P, PACK, E], F32, name="g_raw")
+        for t in range(2):
+            nc.sync.dma_start(out=v_pool[t][:], in_=vals_planes[t])
+        nc.sync.dma_start(out=g_raw[:], in_=grows.rearrange("(p j) e -> p j e", j=PACK))
+        for t in range(2, 4):
+            nc.sync.dma_start(out=v_pool[t][:], in_=vals_planes[t])
+        old_sb = sb.tile([P, PACK, I], F32, name="old_sb")
+        nc.sync.dma_start(out=old_sb[:], in_=old.rearrange("(p t) i -> p t i", t=PACK))
+
+        ident = sb.tile([P, P], F32, name="ident")
+        make_identity(nc, ident[:])
+        sg_rows = ps.tile([P, 2, P], F32, name="sg_rows")
+        for m in range(2):
+            nc.tensor.transpose(sg_rows[:, m, :], sg_cols[:, m : m + 1].to_broadcast([P, P]), ident[:])
+
+        kg_bytes = sb.tile([P, I], U8, name="kg_bytes", align_bytes=64)
+        nc.vector.tensor_copy(kg_bytes[:], k_bytes[:].indirect(offsets[:]))
+
+        q_bf = sb.tile([P, Q * PACK], BF16, name="q_bf", align_bytes=64)
+        deal(nc.vector.tensor_copy, q_bf, q_raw, 0, QUERY_SPLIT)
+        deal(nc.scalar.copy, q_bf, q_raw, QUERY_SPLIT, P)
+        q_codes = sb.tile([P, Q], U32, name="q_codes", align_bytes=64)
+        q_scales = sb.tile([P, Q], U8, name="q_scales", align_bytes=64)
+        nc.vector.quantize_mx(out=q_codes[:].bitcast(FP8X4), scales=q_scales[:], in_=q_bf[:])
+
+        kg_words = sb.tile([P, I], U32, name="kg_words", align_bytes=64)
+        nc.vector.tensor_copy(kg_words[:], k_words[:].bitcast(U32).indirect(offsets[:]))
+
+        scores = []
+        for r in range(PACK):
+            bank = ps.tile([P, I], F32, name=f"scores{r}", tag=f"bank{r}")
+            cols = slice(r * P, (r + 1) * P)
+            nc.tensor.matmul_mx(
+                out=bank[:], lhsT=q_codes[:, cols].bitcast(FP8X4), lhsT_scale=q_scales[:, cols],
+                rhs=kg_words[:].bitcast(FP8X4), rhs_scale=kg_bytes[:], start=True, stop=True,
+            )
+            scores.append(bank)
+
+        x_g = [sb.tile([P, I], F32, name=f"x_g{t}") for t in range(PACK)]
+        th = [sb.tile([P, I], F32, name=f"th{t}") for t in range(PACK)]
+        th2 = [sb.tile([P, I], F32, name=f"th2_{t}") for t in range(PACK)]
+        fac = [sb.tile([P, I], F32, name=f"fac{t}") for t in range(PACK)]
+
+        def gather_plane(t):
+            nc.vector.tensor_copy(x_g[t][:], v_pool[t][:].indirect(offsets[:]))
+
+        def tanh_squared(t):
+            nc.scalar.activation(out=th[t][:], in_=x_g[t][:], func=ACT.Tanh, scale=gain_sb[:, t : t + 1])
+            nc.scalar.activation(out=th2[t][:], in_=th[t][:], func=ACT.Square)
+
+        def factor(t):
+            nc.vector.scalar_tensor_tensor(
+                out=fac[t][:].rearrange("p (n m) -> p n m", m=2), in0=th2[t][:].rearrange("p (n m) -> p n m", m=2), scalar=1.0,
+                in1=sg_rows[:].rearrange("p m n -> p n m"), op0=ALU.subtract, op1=ALU.mult,
+            )
+
+        gather_plane(0)
+        neg_max = [sb.tile([P, 1], F32, name=f"neg_max{r}") for r in range(PACK)]
+        row_sum = [sb.tile([P, 2], F32, name=f"row_sum{h}") for h in range(2)]
+        inv_sum = [sb.tile([P, 2], F32, name=f"inv_sum{h}") for h in range(2)]
+        row_scale = sb.tile([P, 2], F32, name="row_scale")
+        p_exp = [sb.tile([P, I], F32, name=f"p_exp{r}") for r in range(PACK)]
+        w_rows = sb.tile([P, PACK * I], BF16, name="w_rows")
+        for r in range(PACK):
+            nc.vector.tensor_reduce(out=neg_max[r][:], in_=scores[r][:], axis=AX.X, op=ALU.max, negate=True)
+            nc.scalar.activation(
+                out=p_exp[r][:], in_=scores[r][:], func=ACT.Exp, bias=neg_max[r][:],
+                accum_out=row_sum[r // 2][:, r % 2 : r % 2 + 1],
+            )
+        nc.vector.reciprocal(out=inv_sum[0][:], in_=row_sum[0][:])
+        gather_plane(1)
+        nc.vector.tensor_tensor(out=row_scale[:], in0=inv_sum[0][:], in1=qs_sb[:, 0:2], op=ALU.mult)
+        nc.vector.reciprocal(out=inv_sum[1][:], in_=row_sum[1][:])
+        for r in range(2):
+            nc.scalar.activation(out=w_rows[:, r * I : (r + 1) * I], in_=p_exp[r][:], func=ACT.Copy, scale=row_scale[:, r : r + 1])
+        for r in range(2, PACK):
+            nc.vector.tensor_scalar(
+                out=w_rows[:, r * I : (r + 1) * I], in0=p_exp[r][:], scalar1=inv_sum[1][:, r - 2 : r - 1], scalar2=qs_sb[:, r : r + 1],
+                op0=ALU.mult, op1=ALU.mult,
+            )
+        w_bf = sb.tile([P, I * PACK], BF16, name="w_bf", align_bytes=64)
+        nc.vector.tensor_copy(
+            out=w_bf[:].rearrange("p (c i r) -> p c r i", i=4, r=PACK),
+            in_=w_rows[:].rearrange("p (r c i) -> p c r i", r=PACK, i=4),
+        )
+
+        g_bf = sb.tile([P, E * PACK], BF16, name="g_bf", align_bytes=64)
+        deal(nc.scalar.copy, g_bf, g_raw, GROWS_SPLIT, P)
+        deal(nc.vector.tensor_copy, g_bf, g_raw, 0, GROWS_SPLIT)
+
+        w_codes = sb.tile([P, I], U32, name="w_codes", align_bytes=64)
+        w_scales = sb.tile([P, I], U8, name="w_scales", align_bytes=64)
+        nc.vector.quantize_mx(out=w_codes[:].bitcast(FP8X4), scales=w_scales[:], in_=w_bf[:])
+        gather_plane(2)
+        g_codes = sb.tile([P, E], U32, name="g_codes", align_bytes=64)
+        g_scales = sb.tile([P, E], U8, name="g_scales", align_bytes=64)
+        nc.vector.quantize_mx(out=g_codes[:].bitcast(FP8X4), scales=g_scales[:], in_=g_bf[:])
+
+        grads = [ps.tile([P, I], F32, name=f"grad{t}", tag=f"bank{t}") for t in range(PACK)]
+        for t in range(PACK):
+            cols = slice(t * P, (t + 1) * P)
+            nc.tensor.matmul_mx(
+                out=grads[t][:], lhsT=g_codes[:, cols].bitcast(FP8X4), lhsT_scale=g_scales[:, cols],
+                rhs=w_codes[:].bitcast(FP8X4), rhs_scale=w_scales[:], start=True, stop=True,
+            )
+        gather_plane(3)
+        for t in range(PACK):
+            tanh_squared(t)
+
+        y = sb.tile([P, PACK * I], F32, name="y")
+        out_planes = out_0.rearrange("(p t) i -> p (t i)", t=PACK)
+        prod = [sb.tile([P, I], F32, name=f"prod{t}") for t in range(PACK)]
+        def product(t):
+            nc.vector.tensor_tensor(out=prod[t][:], in0=grads[t][:], in1=fac[t][:], op=ALU.mult)
+
+        def add_old(t, engine):
+            engine.tensor_tensor(out=y[:, t * I : (t + 1) * I], in0=old_sb[:, t, :], in1=prod[t][:], op=ALU.subtract)
+
+        factor(0)
+        factor(1)
+        product(0)
+        add_old(0, nc.gpsimd)
+        product(1)
+        add_old(1, nc.gpsimd)
+        nc.sync.dma_start(out=out_planes[:, 0 : 2 * I], in_=y[:, 0 : 2 * I])
+        factor(2)
+        factor(3)
+        product(2)
+        add_old(2, nc.gpsimd)
+        product(3)
+        add_old(3, nc.vector)
+        nc.sync.dma_start(out=out_planes[:, 2 * I :], in_=y[:, 2 * I :])
+
+        y_bf = sb.tile([P, I * PACK], BF16, name="y_bf", align_bytes=64)
+        y_dst = y_bf[:].rearrange("p (c i t) -> p c t i", i=4, t=PACK)
+        y_src = y[:].rearrange("p (t c i) -> p c t i", t=PACK, i=4)
+        nc.vector.tensor_copy(out=y_dst[:, :OUT_SPLIT], in_=y_src[:, :OUT_SPLIT])
+        nc.scalar.copy(out=y_dst[:, OUT_SPLIT:], in_=y_src[:, OUT_SPLIT:])
+        y_codes = sb.tile([P, I], I32, name="y_codes", align_bytes=64)
+        y_scales = sb.tile([P, I], U8, name="y_scales", align_bytes=64)
+        nc.vector.quantize_mx(out=y_codes[:].bitcast(FP8X4), scales=y_scales[:], in_=y_bf[:])
+        nc.sync.dma_start(out=out_1[0].rearrange("p n t -> p (n t)").bitcast(I32), in_=y_codes[:])
+        for quad in range(4):
+            queue = nc.scalar if quad % 2 == 0 else nc.sync
+            queue.dma_start(
+                out=out_2[0, 4 * quad : 4 * quad + 4, :].bitcast(I32),
+                in_=y_scales[32 * quad : 32 * quad + 4, :].bitcast(I32),
+            )

@@ -20,14 +20,14 @@ AX = mybir.AxisListType
 P = 128
 PACK = 4
 QUERY_SPLIT = 84
-GROWS_SPLIT = 24
+GROWS_SPLIT = 32
 OUT_SPLIT = 42
 
 
-def deal(copy, dst, src, lo, hi):
+def deal(copy, dst, src, half):
     copy(
-        out=dst[:].rearrange("p (r s j) -> p s r j", r=PACK, j=PACK)[:, lo:hi],
-        in_=src[:].rearrange("p j (s r) -> p s r j", r=PACK)[:, lo:hi],
+        out=dst[:].rearrange("p (r s j) -> p s j r", r=2, j=PACK),
+        in_=src[:].rearrange("p j (s r) -> p s j r", r=PACK)[:, :, :, 2 * half : 2 * half + 2],
     )
 
 
@@ -61,11 +61,12 @@ def tile_attend_bvtanh_d_pl_kernel(tc, query, qs, grows, vals, keys_words, keys_
         qs_sb = sb.tile([P, PACK], F32, name="qs_sb")
         nc.gpsimd.dma_start(out=qs_sb[:], in_=qs.rearrange("(p r) o -> p (r o)", r=PACK))
         sg_cols = sb.tile([P, 2], F32, name="sg_cols")
-        nc.gpsimd.dma_start(out=sg_cols[:], in_=sg.rearrange("o (n m) -> n (o m)", m=2))
+        with nc.allow_non_contiguous_dma(reason="one value a partition"):
+            nc.gpsimd.dma_start(out=sg_cols[:], in_=sg.rearrange("o (m n) -> n (o m)", m=2))
 
         vals_planes = vals.rearrange("(p t) x -> t p x", t=PACK)
-        v_pool = [sb.tile([P, T], F32, name=f"v_pool{t}") for t in range(PACK)]
-        g_raw = sb.tile([P, PACK, E], F32, name="g_raw")
+        v_pool = [sb.tile([P, T], F32, name=f"v_pool{t}", tag=f"v_pool{t}") for t in range(PACK)]
+        g_raw = sb.tile([P, PACK, E], F32, name="g_raw", tag="g_raw")
         for t in range(2):
             nc.sync.dma_start(out=v_pool[t][:], in_=vals_planes[t])
         nc.sync.dma_start(out=g_raw[:], in_=grows.rearrange("(p j) e -> p j e", j=PACK))
@@ -76,127 +77,119 @@ def tile_attend_bvtanh_d_pl_kernel(tc, query, qs, grows, vals, keys_words, keys_
 
         ident = sb.tile([P, P], F32, name="ident")
         make_identity(nc, ident[:])
-        sg_rows = ps.tile([P, 2, P], F32, name="sg_rows")
-        for m in range(2):
-            nc.tensor.transpose(sg_rows[:, m, :], sg_cols[:, m : m + 1].to_broadcast([P, P]), ident[:])
 
         kg_bytes = sb.tile([P, I], U8, name="kg_bytes", align_bytes=64)
         nc.vector.tensor_copy(kg_bytes[:], k_bytes[:].indirect(offsets[:]))
 
-        q_bf = sb.tile([P, Q * PACK], BF16, name="q_bf", align_bytes=64)
-        deal(nc.vector.tensor_copy, q_bf, q_raw, 0, QUERY_SPLIT)
-        deal(nc.scalar.copy, q_bf, q_raw, QUERY_SPLIT, P)
-        q_codes = sb.tile([P, Q], U32, name="q_codes", align_bytes=64)
-        q_scales = sb.tile([P, Q], U8, name="q_scales", align_bytes=64)
-        nc.vector.quantize_mx(out=q_codes[:].bitcast(FP8X4), scales=q_scales[:], in_=q_bf[:])
-
+        q_bf = [sb.tile([P, 2 * P * PACK], BF16, name=f"q_bf{h}", align_bytes=64) for h in range(2)]
+        q_codes = [sb.tile([P, 2 * P], U32, name=f"q_codes{h}", align_bytes=64) for h in range(2)]
+        q_scales = [sb.tile([P, 2 * P], U8, name=f"q_scales{h}", align_bytes=64) for h in range(2)]
+        deal(nc.vector.tensor_copy, q_bf[0], q_raw, 0)
+        deal(nc.scalar.copy, q_bf[1], q_raw, 1)
+        nc.vector.quantize_mx(out=q_codes[0][:].bitcast(FP8X4), scales=q_scales[0][:], in_=q_bf[0][:])
         kg_words = sb.tile([P, I], U32, name="kg_words", align_bytes=64)
         nc.vector.tensor_copy(kg_words[:], k_words[:].bitcast(U32).indirect(offsets[:]))
+        nc.vector.quantize_mx(out=q_codes[1][:].bitcast(FP8X4), scales=q_scales[1][:], in_=q_bf[1][:])
 
         scores = []
         for r in range(PACK):
             bank = ps.tile([P, I], F32, name=f"scores{r}", tag=f"bank{r}")
-            cols = slice(r * P, (r + 1) * P)
+            cols = slice((r % 2) * P, (r % 2 + 1) * P)
             nc.tensor.matmul_mx(
-                out=bank[:], lhsT=q_codes[:, cols].bitcast(FP8X4), lhsT_scale=q_scales[:, cols],
+                out=bank[:], lhsT=q_codes[r // 2][:, cols].bitcast(FP8X4), lhsT_scale=q_scales[r // 2][:, cols],
                 rhs=kg_words[:].bitcast(FP8X4), rhs_scale=kg_bytes[:], start=True, stop=True,
             )
             scores.append(bank)
 
-        x_g = [sb.tile([P, I], F32, name=f"x_g{t}") for t in range(PACK)]
-        th = [sb.tile([P, I], F32, name=f"th{t}") for t in range(PACK)]
-        th2 = [sb.tile([P, I], F32, name=f"th2_{t}") for t in range(PACK)]
-        fac = [sb.tile([P, I], F32, name=f"fac{t}") for t in range(PACK)]
+        picked = []
 
-        def gather_plane(t):
-            nc.vector.tensor_copy(x_g[t][:], v_pool[t][:].indirect(offsets[:]))
+        def gather(t, tag):
+            picked.append(sb.tile([P, I], F32, name=f"picked{t}", tag=tag))
+            nc.vector.tensor_copy(picked[t][:], v_pool[t][:].indirect(offsets[:]))
 
-        def tanh_squared(t):
-            nc.scalar.activation(out=th[t][:], in_=x_g[t][:], func=ACT.Tanh, scale=gain_sb[:, t : t + 1])
-            nc.scalar.activation(out=th2[t][:], in_=th[t][:], func=ACT.Square)
+        def tanh(t, out):
+            nc.scalar.activation(out=out, in_=picked[t][:], func=ACT.Tanh, scale=gain_sb[:, t : t + 1])
 
-        def factor(t):
-            nc.vector.scalar_tensor_tensor(
-                out=fac[t][:].rearrange("p (n m) -> p n m", m=2), in0=th2[t][:].rearrange("p (n m) -> p n m", m=2), scalar=1.0,
-                in1=sg_rows[:].rearrange("p m n -> p n m"), op0=ALU.subtract, op1=ALU.mult,
-            )
-
-        gather_plane(0)
-        neg_max = [sb.tile([P, 1], F32, name=f"neg_max{r}") for r in range(PACK)]
+        th0 = sb.tile([P, I], F32, name="th0")
+        gather(0, "picked0")
+        tanh(0, th0[:])
+        neg_max = [sb.tile([P, 1], F32, name=f"neg_max{r}", tag=f"neg_max{r}") for r in range(PACK)]
         row_sum = [sb.tile([P, 2], F32, name=f"row_sum{h}") for h in range(2)]
         inv_sum = [sb.tile([P, 2], F32, name=f"inv_sum{h}") for h in range(2)]
-        row_scale = sb.tile([P, 2], F32, name="row_scale")
         p_exp = [sb.tile([P, I], F32, name=f"p_exp{r}") for r in range(PACK)]
-        w_rows = sb.tile([P, PACK * I], BF16, name="w_rows")
+        w_rows = sb.tile([P, PACK, I], BF16, name="w_rows")
         for r in range(PACK):
             nc.vector.tensor_reduce(out=neg_max[r][:], in_=scores[r][:], axis=AX.X, op=ALU.max, negate=True)
             nc.scalar.activation(
                 out=p_exp[r][:], in_=scores[r][:], func=ACT.Exp, bias=neg_max[r][:],
                 accum_out=row_sum[r // 2][:, r % 2 : r % 2 + 1],
             )
-        nc.vector.reciprocal(out=inv_sum[0][:], in_=row_sum[0][:])
-        gather_plane(1)
-        nc.vector.tensor_tensor(out=row_scale[:], in0=inv_sum[0][:], in1=qs_sb[:, 0:2], op=ALU.mult)
-        nc.vector.reciprocal(out=inv_sum[1][:], in_=row_sum[1][:])
-        for r in range(2):
-            nc.scalar.activation(out=w_rows[:, r * I : (r + 1) * I], in_=p_exp[r][:], func=ACT.Copy, scale=row_scale[:, r : r + 1])
-        for r in range(2, PACK):
-            nc.vector.tensor_scalar(
-                out=w_rows[:, r * I : (r + 1) * I], in0=p_exp[r][:], scalar1=inv_sum[1][:, r - 2 : r - 1], scalar2=qs_sb[:, r : r + 1],
-                op0=ALU.mult, op1=ALU.mult,
-            )
+        sg_rows = ps.tile([P, 2 * P], F32, name="sg_rows", tag="bank0")
+        for m in range(2):
+            nc.tensor.transpose(sg_rows[:, m * P : (m + 1) * P], sg_cols[:, m : m + 1].to_broadcast([P, P]), ident[:])
+        for h in range(2):
+            nc.vector.reciprocal(out=inv_sum[h][:], in_=row_sum[h][:])
+            if h == 0:
+                gather(1, "neg_max1")
+            for r in (2 * h, 2 * h + 1):
+                nc.vector.tensor_scalar(
+                    out=w_rows[:, r, :], in0=p_exp[r][:], scalar1=inv_sum[h][:, r % 2 : r % 2 + 1],
+                    scalar2=qs_sb[:, r : r + 1], op0=ALU.mult, op1=ALU.mult,
+                )
         w_bf = sb.tile([P, I * PACK], BF16, name="w_bf", align_bytes=64)
         nc.vector.tensor_copy(
             out=w_bf[:].rearrange("p (c i r) -> p c r i", i=4, r=PACK),
-            in_=w_rows[:].rearrange("p (r c i) -> p c r i", r=PACK, i=4),
+            in_=w_rows[:].rearrange("p r (c i) -> p c r i", i=4),
         )
 
         g_bf = sb.tile([P, E * PACK], BF16, name="g_bf", align_bytes=64)
-        deal(nc.scalar.copy, g_bf, g_raw, GROWS_SPLIT, P)
-        deal(nc.vector.tensor_copy, g_bf, g_raw, 0, GROWS_SPLIT)
-
+        nc.scalar.copy(
+            out=g_bf[:].rearrange("p (t m j) -> p m j t", t=PACK, j=PACK),
+            in_=g_raw[:].rearrange("p j (m t) -> p m j t", t=PACK),
+        )
+        late = sb.tile([P, 7, I], F32, name="late", tag="g_raw")
+        th2 = [late[:, 3:5, :], late[:, 5:7, :]]
+        tanh(1, late[:, 0, :])
+        nc.scalar.activation(out=th2[0][:, 0, :], in_=th0[:], func=ACT.Square)
+        nc.scalar.activation(out=th2[0][:, 1, :], in_=late[:, 0, :], func=ACT.Square)
+        gather(2, "picked2")
+        tanh(2, late[:, 1, :])
         w_codes = sb.tile([P, I], U32, name="w_codes", align_bytes=64)
         w_scales = sb.tile([P, I], U8, name="w_scales", align_bytes=64)
         nc.vector.quantize_mx(out=w_codes[:].bitcast(FP8X4), scales=w_scales[:], in_=w_bf[:])
-        gather_plane(2)
+        gather(3, "picked3")
+        tanh(3, late[:, 2, :])
+        nc.scalar.activation(out=th2[1], in_=late[:, 1:3, :], func=ACT.Square)
         g_codes = sb.tile([P, E], U32, name="g_codes", align_bytes=64)
         g_scales = sb.tile([P, E], U8, name="g_scales", align_bytes=64)
         nc.vector.quantize_mx(out=g_codes[:].bitcast(FP8X4), scales=g_scales[:], in_=g_bf[:])
 
-        grads = [ps.tile([P, I], F32, name=f"grad{t}", tag=f"bank{t}") for t in range(PACK)]
+        grads = [ps.tile([P, 2, I], F32, name=f"grad{h}") for h in range(2)]
         for t in range(PACK):
             cols = slice(t * P, (t + 1) * P)
             nc.tensor.matmul_mx(
-                out=grads[t][:], lhsT=g_codes[:, cols].bitcast(FP8X4), lhsT_scale=g_scales[:, cols],
+                out=grads[t // 2][:, t % 2, :], lhsT=g_codes[:, cols].bitcast(FP8X4), lhsT_scale=g_scales[:, cols],
                 rhs=w_codes[:].bitcast(FP8X4), rhs_scale=w_scales[:], start=True, stop=True,
             )
-        gather_plane(3)
-        for t in range(PACK):
-            tanh_squared(t)
 
+        fac = sb.tile([P, PACK, I], F32, name="fac")
         y = sb.tile([P, PACK * I], F32, name="y")
         out_planes = out_0.rearrange("(p t) i -> p (t i)", t=PACK)
-        prod = [sb.tile([P, I], F32, name=f"prod{t}") for t in range(PACK)]
-        def product(t):
-            nc.vector.tensor_tensor(out=prod[t][:], in0=grads[t][:], in1=fac[t][:], op=ALU.mult)
-
-        def add_old(t, engine):
-            engine.tensor_tensor(out=y[:, t * I : (t + 1) * I], in0=old_sb[:, t, :], in1=prod[t][:], op=ALU.subtract)
-
-        factor(0)
-        factor(1)
-        product(0)
-        add_old(0, nc.gpsimd)
-        product(1)
-        add_old(1, nc.gpsimd)
-        nc.sync.dma_start(out=out_planes[:, 0 : 2 * I], in_=y[:, 0 : 2 * I])
-        factor(2)
-        factor(3)
-        product(2)
-        add_old(2, nc.gpsimd)
-        product(3)
-        add_old(3, nc.vector)
-        nc.sync.dma_start(out=out_planes[:, 2 * I :], in_=y[:, 2 * I :])
+        prod = [sb.tile([P, 2, I], F32, name=f"prod{h}") for h in range(2)]
+        for h in range(2):
+            nc.vector.scalar_tensor_tensor(
+                out=fac[:, 2 * h : 2 * h + 2, :], in0=th2[h], scalar=1.0,
+                in1=sg_rows[:].unsqueeze(1).to_broadcast([P, 2, I]), op0=ALU.subtract, op1=ALU.mult,
+            )
+        for h in range(2):
+            nc.vector.tensor_tensor(out=prod[h][:], in0=grads[h][:], in1=fac[:, 2 * h : 2 * h + 2, :], op=ALU.mult)
+        for h in range(2):
+            cols = slice(2 * h * I, (2 * h + 2) * I)
+            nc.vector.tensor_tensor(
+                out=y[:, cols], in0=old_sb[:].rearrange("p t i -> p (t i)")[:, cols],
+                in1=prod[h][:].rearrange("p t i -> p (t i)"), op=ALU.subtract,
+            )
+            nc.sync.dma_start(out=out_planes[:, cols], in_=y[:, cols])
 
         y_bf = sb.tile([P, I * PACK], BF16, name="y_bf", align_bytes=64)
         y_dst = y_bf[:].rearrange("p (c i t) -> p c t i", i=4, t=PACK)

@@ -39,22 +39,17 @@ def tile_attend_bvtanh_d_pl_kernel(tc, query, qs, grows, vals, keys_words, keys_
 
         k_bytes = sb.tile([P, T], U8, name="k_bytes", align_bytes=64)
         nc.gpsimd.memset(k_bytes[:].bitcast(I32), 0)
+        q_raw = sb.tile([P, PACK, Q], F32, name="q_raw")
+        nc.sync.dma_start(out=q_raw[:], in_=query.rearrange("(p j) q -> p j q", j=PACK))
         offsets = sb.tile([P, I // 16], U16, name="offsets")
         nc.sync.dma_start(offsets[:], offs)
         for quad in range(4):
-            nc.scalar.dma_start(
+            nc.sync.dma_start(
                 out=k_bytes[32 * quad : 32 * quad + 4, :].bitcast(I32),
                 in_=keys_scales[0, 4 * quad : 4 * quad + 4, :].bitcast(I32),
             )
-        q_raw = sb.tile([P, PACK, Q], F32, name="q_raw")
-        nc.sync.dma_start(out=q_raw[:], in_=query.rearrange("(p j) q -> p j q", j=PACK))
         k_words = sb.tile([P, T], I32, name="k_words", align_bytes=64)
         nc.sync.dma_start(out=k_words[:], in_=keys_words[0].rearrange("p n t -> p (n t)").bitcast(I32))
-
-        warm = sb.tile([P, 1], F32, name="warm")
-        warm2 = sb.tile([P, 1], F32, name="warm2")
-        nc.vector.memset(warm[:], 0.0)
-        nc.scalar.activation(out=warm2[:], in_=warm[:], func=ACT.Exp)
 
         gain_sb = sb.tile([P, PACK], F32, name="gain_sb")
         nc.gpsimd.dma_start(out=gain_sb[:], in_=gain.rearrange("(p t) o -> p (t o)", t=PACK))

@@ -62,10 +62,10 @@ def tile_attend_bvtanh_d_pl_kernel(tc, query, qs, grows, vals, keys_words, keys_
         vals_planes = vals.rearrange("(p t) x -> t p x", t=PACK)
         v_pool = [sb.tile([P, T], F32, name=f"v_pool{t}", tag=f"v_pool{t}") for t in range(PACK)]
         g_raw = sb.tile([P, PACK, E], F32, name="g_raw", tag="g_raw")
-        for t in range(2):
+        for t in range(3):
             nc.sync.dma_start(out=v_pool[t][:], in_=vals_planes[t])
         nc.sync.dma_start(out=g_raw[:], in_=grows.rearrange("(p j) e -> p j e", j=PACK))
-        for t in range(2, 4):
+        for t in range(3, 4):
             nc.sync.dma_start(out=v_pool[t][:], in_=vals_planes[t])
         old_sb = sb.tile([P, PACK, I], F32, name="old_sb")
         nc.sync.dma_start(out=old_sb[:], in_=old.rearrange("(p t) i -> p t i", t=PACK))
@@ -105,9 +105,9 @@ def tile_attend_bvtanh_d_pl_kernel(tc, query, qs, grows, vals, keys_words, keys_
         def tanh(t, out):
             nc.scalar.activation(out=out, in_=picked[t][:], func=ACT.Tanh, scale=gain_sb[:, t : t + 1])
 
-        th0 = sb.tile([P, I], F32, name="th0")
+        th01 = sb.tile([P, 2, I], F32, name="th01")
         gather(0, "picked0")
-        tanh(0, th0[:])
+        tanh(0, th01[:, 0, :])
         neg_max = [sb.tile([P, 1], F32, name=f"neg_max{r}", tag=f"neg_max{r}") for r in range(PACK)]
         row_sum = [sb.tile([P, 2], F32, name=f"row_sum{h}") for h in range(2)]
         inv_sum = [sb.tile([P, 2], F32, name=f"inv_sum{h}") for h in range(2)]
@@ -124,8 +124,7 @@ def tile_attend_bvtanh_d_pl_kernel(tc, query, qs, grows, vals, keys_words, keys_
             nc.tensor.transpose(sg_rows[:, m * P : (m + 1) * P], sg_cols[:, m : m + 1].to_broadcast([P, P]), ident[:])
         for h in range(2):
             nc.vector.reciprocal(out=inv_sum[h][:], in_=row_sum[h][:])
-            if h == 0:
-                gather(1, "neg_max1")
+            gather(1 + h, f"neg_max{2 * h + 1}")
             for r in (2 * h, 2 * h + 1):
                 nc.vector.tensor_scalar(
                     out=w_rows[:, r, :], in0=p_exp[r][:], scalar1=inv_sum[h][:, r % 2 : r % 2 + 1],
@@ -142,19 +141,17 @@ def tile_attend_bvtanh_d_pl_kernel(tc, query, qs, grows, vals, keys_words, keys_
             out=g_bf[:].rearrange("p (t m j) -> p m j t", t=PACK, j=PACK),
             in_=g_raw[:].rearrange("p j (m t) -> p m j t", t=PACK),
         )
-        late = sb.tile([P, 7, I], F32, name="late", tag="g_raw")
-        th2 = [late[:, 3:5, :], late[:, 5:7, :]]
-        tanh(1, late[:, 0, :])
-        nc.scalar.activation(out=th2[0][:, 0, :], in_=th0[:], func=ACT.Square)
-        nc.scalar.activation(out=th2[0][:, 1, :], in_=late[:, 0, :], func=ACT.Square)
-        gather(2, "picked2")
-        tanh(2, late[:, 1, :])
+        late = sb.tile([P, 6, I], F32, name="late", tag="g_raw")
+        th2 = [late[:, 2:4, :], late[:, 4:6, :]]
+        tanh(1, th01[:, 1, :])
+        nc.scalar.activation(out=th2[0], in_=th01[:], func=ACT.Square)
+        tanh(2, late[:, 0, :])
         w_codes = sb.tile([P, I], U32, name="w_codes", align_bytes=64)
         w_scales = sb.tile([P, I], U8, name="w_scales", align_bytes=64)
         nc.vector.quantize_mx(out=w_codes[:].bitcast(FP8X4), scales=w_scales[:], in_=w_bf[:])
         gather(3, "picked3")
-        tanh(3, late[:, 2, :])
-        nc.scalar.activation(out=th2[1], in_=late[:, 1:3, :], func=ACT.Square)
+        tanh(3, late[:, 1, :])
+        nc.scalar.activation(out=th2[1], in_=late[:, 0:2, :], func=ACT.Square)
         g_codes = sb.tile([P, E], U32, name="g_codes", align_bytes=64)
         g_scales = sb.tile([P, E], U8, name="g_scales", align_bytes=64)
         nc.vector.quantize_mx(out=g_codes[:].bitcast(FP8X4), scales=g_scales[:], in_=g_bf[:])
@@ -178,22 +175,25 @@ def tile_attend_bvtanh_d_pl_kernel(tc, query, qs, grows, vals, keys_words, keys_
             )
         for h in range(2):
             nc.vector.tensor_tensor(out=prod[h][:], in0=grads[h][:], in1=fac[:, 2 * h : 2 * h + 2, :], op=ALU.mult)
-        for h in range(2):
-            cols = slice(2 * h * I, (2 * h + 2) * I)
-            nc.vector.tensor_tensor(
-                out=y[:, cols], in0=old_sb[:].rearrange("p t i -> p (t i)")[:, cols],
-                in1=prod[h][:].rearrange("p t i -> p (t i)"), op=ALU.subtract,
-            )
-            nc.sync.dma_start(out=out_planes[:, cols], in_=y[:, cols])
+        y_planes = y[:].rearrange("p (t i) -> p t i", t=PACK)
+        nc.vector.tensor_tensor(out=y_planes[:, 0:2, :], in0=old_sb[:, 0:2, :], in1=prod[0][:], op=ALU.subtract)
+        nc.sync.dma_start(out=out_planes[:, : 2 * I], in_=y[:, : 2 * I])
+        for c in range(2):
+            slots = slice(c * P, (c + 1) * P)
+            nc.vector.tensor_tensor(out=y_planes[:, 2:4, slots], in0=old_sb[:, 2:4, slots], in1=prod[1][:, :, slots], op=ALU.subtract)
+        nc.sync.dma_start(out=out_planes[:, 2 * I :], in_=y[:, 2 * I :])
 
-        y_bf = sb.tile([P, I * PACK], BF16, name="y_bf", align_bytes=64)
-        y_dst = y_bf[:].rearrange("p (c i t) -> p c t i", i=4, t=PACK)
-        y_src = y[:].rearrange("p (t c i) -> p c t i", t=PACK, i=4)
-        nc.vector.tensor_copy(out=y_dst[:, :OUT_SPLIT], in_=y_src[:, :OUT_SPLIT])
-        nc.scalar.copy(out=y_dst[:, OUT_SPLIT:], in_=y_src[:, OUT_SPLIT:])
+        y_bf = [sb.tile([P, P * PACK], BF16, name=f"y_bf{c}", align_bytes=64) for c in range(2)]
         y_codes = sb.tile([P, I], I32, name="y_codes", align_bytes=64)
         y_scales = sb.tile([P, I], U8, name="y_scales", align_bytes=64)
-        nc.vector.quantize_mx(out=y_codes[:].bitcast(FP8X4), scales=y_scales[:], in_=y_bf[:])
+        for c, copy in enumerate((nc.scalar.copy, nc.vector.tensor_copy)):
+            copy(
+                out=y_bf[c][:].rearrange("p (n i t) -> p n t i", i=4, t=PACK),
+                in_=y_planes[:, :, c * P : (c + 1) * P].rearrange("p t (n i) -> p n t i", i=4),
+            )
+        for c in range(2):
+            slots = slice(c * P, (c + 1) * P)
+            nc.vector.quantize_mx(out=y_codes[:, slots].bitcast(FP8X4), scales=y_scales[:, slots], in_=y_bf[c][:])
         nc.sync.dma_start(out=out_1[0].rearrange("p n t -> p (n t)").bitcast(I32), in_=y_codes[:])
         for quad in range(4):
             queue = nc.scalar if quad % 2 == 0 else nc.sync

from contextlib import ExitStack

import concourse.mybir as mybir
from concourse.masks import make_identity

D, E, T, I, Q = 512, 512, 1024, 256, 512
FLOPS = 2 * D * Q * I + 2 * Q * E * I

F32 = mybir.dt.float32
BF16 = mybir.dt.bfloat16
I32 = mybir.dt.int32
U32 = mybir.dt.uint32
U16 = mybir.dt.uint16
U8 = mybir.dt.uint8
FP8X4 = mybir.dt.float8_e4m3fn_x4
ALU = mybir.AluOpType
ACT = mybir.ActivationFunctionType
AX = mybir.AxisListType

P = 128
PACK = 4
QUERY_SPLIT = 84
GROWS_SPLIT = 32
OUT_SPLIT = 42


def deal(copy, dst, src, half):
    copy(
        out=dst[:].rearrange("p (r s j) -> p s j r", r=2, j=PACK),
        in_=src[:].rearrange("p j (s r) -> p s j r", r=PACK)[:, :, :, 2 * half : 2 * half + 2],
    )


def tile_attend_bvtanh_d_pl_kernel(tc, query, qs, grows, vals, keys_words, keys_scales, gain, sg, old, offs, out_0, out_1, out_2):
    nc = tc.nc
    with ExitStack() as ctx:
        sb = ctx.enter_context(tc.tile_pool(name="sb", bufs=1))
        ps = ctx.enter_context(tc.psum_pool(name="ps", bufs=1))

        k_bytes = sb.tile([P, T], U8, name="k_bytes", align_bytes=64)
        nc.gpsimd.memset(k_bytes[:].bitcast(I32), 0)
        q_raw = sb.tile([P, PACK, Q], F32, name="q_raw")
        nc.sync.dma_start(out=q_raw[:], in_=query.rearrange("(p j) q -> p j q", j=PACK))
        offsets = sb.tile([P, I // 16], U16, name="offsets")
        nc.sync.dma_start(offsets[:], offs)
        for quad in range(4):
            nc.sync.dma_start(
                out=k_bytes[32 * quad : 32 * quad + 4, :].bitcast(I32),
                in_=keys_scales[0, 4 * quad : 4 * quad + 4, :].bitcast(I32),
            )
        k_words = sb.tile([P, T], I32, name="k_words", align_bytes=64)
        nc.sync.dma_start(out=k_words[:], in_=keys_words[0].rearrange("p n t -> p (n t)").bitcast(I32))

        gain_sb = sb.tile([P, PACK], F32, name="gain_sb")
        nc.gpsimd.dma_start(out=gain_sb[:], in_=gain.rearrange("(p t) o -> p (t o)", t=PACK))
        qs_sb = sb.tile([P, PACK], F32, name="qs_sb")
        nc.gpsimd.dma_start(out=qs_sb[:], in_=qs.rearrange("(p r) o -> p (r o)", r=PACK))
        sg_cols = sb.tile([P, 2], F32, name="sg_cols")
        with nc.allow_non_contiguous_dma(reason="one value a partition"):
            nc.gpsimd.dma_start(out=sg_cols[:], in_=sg.rearrange("o (m n) -> n (o m)", m=2))

        vals_planes = vals.rearrange("(p t) x -> t p x", t=PACK)
        v_pool = [sb.tile([P, T], F32, name=f"v_pool{t}", tag=f"v_pool{t}") for t in range(PACK)]
        g_raw = sb.tile([P, PACK, E], F32, name="g_raw", tag="g_raw")
        for t in range(3):
            nc.sync.dma_start(out=v_pool[t][:], in_=vals_planes[t])
        nc.sync.dma_start(out=g_raw[:], in_=grows.rearrange("(p j) e -> p j e", j=PACK))
        for t in range(3, 4):
            nc.sync.dma_start(out=v_pool[t][:], in_=vals_planes[t])
        old_sb = sb.tile([P, PACK, I], F32, name="old_sb")
        nc.sync.dma_start(out=old_sb[:], in_=old.rearrange("(p t) i -> p t i", t=PACK))

        ident = sb.tile([P, P], F32, name="ident")
        make_identity(nc, ident[:])

        kg_bytes = sb.tile([P, I], U8, name="kg_bytes", align_bytes=64)
        nc.vector.tensor_copy(kg_bytes[:], k_bytes[:].indirect(offsets[:]))

        q_bf = [sb.tile([P, 2 * P * PACK], BF16, name=f"q_bf{h}", align_bytes=64) for h in range(2)]
        q_codes = [sb.tile([P, 2 * P], U32, name=f"q_codes{h}", align_bytes=64) for h in range(2)]
        q_scales = [sb.tile([P, 2 * P], U8, name=f"q_scales{h}", align_bytes=64) for h in range(2)]
        deal(nc.vector.tensor_copy, q_bf[0], q_raw, 0)
        deal(nc.scalar.copy, q_bf[1], q_raw, 1)
        nc.vector.quantize_mx(out=q_codes[0][:].bitcast(FP8X4), scales=q_scales[0][:], in_=q_bf[0][:])
        kg_words = sb.tile([P, I], U32, name="kg_words", align_bytes=64)
        nc.vector.tensor_copy(kg_words[:], k_words[:].bitcast(U32).indirect(offsets[:]))
        nc.vector.quantize_mx(out=q_codes[1][:].bitcast(FP8X4), scales=q_scales[1][:], in_=q_bf[1][:])

        scores = []
        for r in range(PACK):
            bank = ps.tile([P, I], F32, name=f"scores{r}", tag=f"bank{r}")
            cols = slice((r % 2) * P, (r % 2 + 1) * P)
            nc.tensor.matmul_mx(
                out=bank[:], lhsT=q_codes[r // 2][:, cols].bitcast(FP8X4), lhsT_scale=q_scales[r // 2][:, cols],
                rhs=kg_words[:].bitcast(FP8X4), rhs_scale=kg_bytes[:], start=True, stop=True,
            )
            scores.append(bank)

        picked = []

        def gather(t, tag):
            picked.append(sb.tile([P, I], F32, name=f"picked{t}", tag=tag))
            nc.vector.tensor_copy(picked[t][:], v_pool[t][:].indirect(offsets[:]))

        def tanh(t, out):
            nc.scalar.activation(out=out, in_=picked[t][:], func=ACT.Tanh, scale=gain_sb[:, t : t + 1])

        th01 = sb.tile([P, 2, I], F32, name="th01")
        gather(0, "picked0")
        tanh(0, th01[:, 0, :])
        neg_max = [sb.tile([P, 1], F32, name=f"neg_max{r}", tag=f"neg_max{r}") for r in range(PACK)]
        row_sum = [sb.tile([P, 2], F32, name=f"row_sum{h}") for h in range(2)]
        inv_sum = [sb.tile([P, 2], F32, name=f"inv_sum{h}") for h in range(2)]
        p_exp = [sb.tile([P, I], F32, name=f"p_exp{r}") for r in range(PACK)]
        w_rows = sb.tile([P, PACK, I], BF16, name="w_rows")
        for r in range(PACK):
            nc.vector.tensor_reduce(out=neg_max[r][:], in_=scores[r][:], axis=AX.X, op=ALU.max, negate=True)
            nc.scalar.activation(
                out=p_exp[r][:], in_=scores[r][:], func=ACT.Exp, bias=neg_max[r][:],
                accum_out=row_sum[r // 2][:, r % 2 : r % 2 + 1],
            )
        sg_rows = ps.tile([P, 2 * P], F32, name="sg_rows", tag="bank0")
        for m in range(2):
            nc.tensor.transpose(sg_rows[:, m * P : (m + 1) * P], sg_cols[:, m : m + 1].to_broadcast([P, P]), ident[:])
        for h in range(2):
            nc.vector.reciprocal(out=inv_sum[h][:], in_=row_sum[h][:])
            gather(1 + h, f"neg_max{2 * h + 1}")
            for r in (2 * h, 2 * h + 1):
                nc.vector.tensor_scalar(
                    out=w_rows[:, r, :], in0=p_exp[r][:], scalar1=inv_sum[h][:, r % 2 : r % 2 + 1],
                    scalar2=qs_sb[:, r : r + 1], op0=ALU.mult, op1=ALU.mult,
                )
        w_bf = sb.tile([P, I * PACK], BF16, name="w_bf", align_bytes=64)
        nc.vector.tensor_copy(
            out=w_bf[:].rearrange("p (c i r) -> p c r i", i=4, r=PACK),
            in_=w_rows[:].rearrange("p r (c i) -> p c r i", i=4),
        )

        g_bf = sb.tile([P, E * PACK], BF16, name="g_bf", align_bytes=64)
        nc.scalar.copy(
            out=g_bf[:].rearrange("p (t m j) -> p m j t", t=PACK, j=PACK),
            in_=g_raw[:].rearrange("p j (m t) -> p m j t", t=PACK),
        )
        late = sb.tile([P, 6, I], F32, name="late", tag="g_raw")
        th2 = [late[:, 2:4, :], late[:, 4:6, :]]
        tanh(1, th01[:, 1, :])
        nc.scalar.activation(out=th2[0], in_=th01[:], func=ACT.Square)
        tanh(2, late[:, 0, :])
        w_codes = sb.tile([P, I], U32, name="w_codes", align_bytes=64)
        w_scales = sb.tile([P, I], U8, name="w_scales", align_bytes=64)
        nc.vector.quantize_mx(out=w_codes[:].bitcast(FP8X4), scales=w_scales[:], in_=w_bf[:])
        gather(3, "picked3")
        tanh(3, late[:, 1, :])
        nc.scalar.activation(out=th2[1], in_=late[:, 0:2, :], func=ACT.Square)
        g_codes = sb.tile([P, E], U32, name="g_codes", align_bytes=64)
        g_scales = sb.tile([P, E], U8, name="g_scales", align_bytes=64)
        nc.vector.quantize_mx(out=g_codes[:].bitcast(FP8X4), scales=g_scales[:], in_=g_bf[:])

        grads = [ps.tile([P, 2, I], F32, name=f"grad{h}") for h in range(2)]
        for t in range(PACK):
            cols = slice(t * P, (t + 1) * P)
            nc.tensor.matmul_mx(
                out=grads[t // 2][:, t % 2, :], lhsT=g_codes[:, cols].bitcast(FP8X4), lhsT_scale=g_scales[:, cols],
                rhs=w_codes[:].bitcast(FP8X4), rhs_scale=w_scales[:], start=True, stop=True,
            )

        fac = sb.tile([P, PACK, I], F32, name="fac")
        y = sb.tile([P, PACK * I], F32, name="y")
        out_planes = out_0.rearrange("(p t) i -> p (t i)", t=PACK)
        prod = [sb.tile([P, 2, I], F32, name=f"prod{h}") for h in range(2)]
        for h in range(2):
            nc.vector.scalar_tensor_tensor(
                out=fac[:, 2 * h : 2 * h + 2, :], in0=th2[h], scalar=1.0,
                in1=sg_rows[:].unsqueeze(1).to_broadcast([P, 2, I]), op0=ALU.subtract, op1=ALU.mult,
            )
        for h in range(2):
            nc.vector.tensor_tensor(out=prod[h][:], in0=grads[h][:], in1=fac[:, 2 * h : 2 * h + 2, :], op=ALU.mult)
        y_planes = y[:].rearrange("p (t i) -> p t i", t=PACK)
        nc.vector.tensor_tensor(out=y_planes[:, 0:2, :], in0=old_sb[:, 0:2, :], in1=prod[0][:], op=ALU.subtract)
        nc.sync.dma_start(out=out_planes[:, : 2 * I], in_=y[:, : 2 * I])
        for c in range(2):
            slots = slice(c * P, (c + 1) * P)
            nc.vector.tensor_tensor(out=y_planes[:, 2:4, slots], in0=old_sb[:, 2:4, slots], in1=prod[1][:, :, slots], op=ALU.subtract)
        nc.sync.dma_start(out=out_planes[:, 2 * I :], in_=y[:, 2 * I :])

        y_bf = [sb.tile([P, P * PACK], BF16, name=f"y_bf{c}", align_bytes=64) for c in range(2)]
        y_codes = sb.tile([P, I], I32, name="y_codes", align_bytes=64)
        y_scales = sb.tile([P, I], U8, name="y_scales", align_bytes=64)
        for c, copy in enumerate((nc.scalar.copy, nc.vector.tensor_copy)):
            copy(
                out=y_bf[c][:].rearrange("p (n i t) -> p n t i", i=4, t=PACK),
                in_=y_planes[:, :, c * P : (c + 1) * P].rearrange("p t (n i) -> p n t i", i=4),
            )
        for c in range(2):
            slots = slice(c * P, (c + 1) * P)
            nc.vector.quantize_mx(out=y_codes[:, slots].bitcast(FP8X4), scales=y_scales[:, slots], in_=y_bf[c][:])
        nc.sync.dma_start(out=out_1[0].rearrange("p n t -> p (n t)").bitcast(I32), in_=y_codes[:])
        for quad in range(4):
            queue = nc.scalar if quad % 2 == 0 else nc.sync
            queue.dma_start(
                out=out_2[0, 4 * quad : 4 * quad + 4, :].bitcast(I32),
                in_=y_scales[32 * quad : 32 * quad + 4, :].bitcast(I32),
            )
